import numpy as np
import ml_dtypes


def mxq(x, axis, fmt="e4m3"):
    dtype, down = {"e4m3": (ml_dtypes.float8_e4m3fn, 7), "e5m2": (ml_dtypes.float8_e5m2, 14)}[fmt]
    v = np.moveaxis(np.asarray(x, np.float32).astype(ml_dtypes.bfloat16).astype(np.float64), axis, -1)
    blocks = v.reshape(v.shape[:-1] + (-1, 32))
    amax = np.abs(blocks).max(-1, keepdims=True)
    byte = np.maximum(np.where(amax > 0, np.frexp(amax)[1] - 1 + 127, 0) - down, 1)
    scale = np.exp2(byte - 127.0)
    codes = (blocks / scale).astype(np.float32).astype(dtype).astype(np.float64)
    return np.moveaxis((codes * scale).reshape(v.shape), -1, axis)


WIDE = False


def mx_kscale(k):
    if not WIDE:
        return np.ones(k)
    levels = np.array([10, -10, 5, -5, 0])
    if k % 512:
        return np.exp2(np.random.permutation(np.resize(levels, k // 32))).repeat(32)
    a = np.empty((k // 512, 16))
    for p in range(k // 512):
        a[p, :8] = np.random.permutation(np.resize(levels, 8))
        for g in range(8):
            far = levels[np.abs(levels - a[p, g]) >= 10]
            a[p, g + 8] = far[np.random.randint(len(far))]
    return np.exp2(a.ravel()).repeat(32)


def f64(x):
    return np.asarray(x).astype(np.float64)


def striped(idx):
    return np.tile(idx.reshape(-1, 16).T, (8, 1)).astype(np.uint16)


def unstriped(offs):
    return offs[:16].T.reshape(-1).astype(np.int64)


E2M1 = np.array([0.0, 0.5, 1.0, 1.5, 2.0, 3.0, 4.0, 6.0, -0.0, -0.5, -1.0, -1.5, -2.0, -3.0, -4.0, -6.0])


def pack_weight(w, fmt):
    k, n = w.shape
    w = f64(np.asarray(w, np.float32).astype(ml_dtypes.bfloat16)).reshape(k // 32, 32, n)
    amax = np.abs(w).max(1)
    if fmt == "e4m3":
        byte = np.frexp(amax)[1] - 1 + 127 - 7
    else:
        mant, ex = np.frexp(amax / 6.0)
        byte = np.where(mant > 0.5, ex, ex - 1) + 127
    byte = np.clip(np.where(amax > 0, byte, 1), 1, 254)
    scaled = (w * np.exp2(127.0 - byte)[:, None, :]).reshape(k, n).astype(np.float32)
    by_word = np.ascontiguousarray(scaled.reshape(k // 512, 128, 4, n).transpose(0, 1, 3, 2))
    if fmt == "e4m3":
        words = by_word.astype(ml_dtypes.float8_e4m3fn).view(np.uint8)
    else:
        c = by_word.astype(ml_dtypes.float4_e2m1fn).view(np.uint8) & 0xF
        words = (c[..., 0::2] | (c[..., 1::2] << 4)).reshape(k // 512, 128, 2 * n)
    return np.ascontiguousarray(words), np.ascontiguousarray(byte.astype(np.uint8).reshape(k // 512, 16, n))


def unpack_weight(words, scales, fmt):
    g, _, n = scales.shape
    words = np.ascontiguousarray(words).reshape(g, 128, n, -1)
    if fmt == "e4m3":
        vals = words.view(ml_dtypes.float8_e4m3fn).astype(np.float64)
    else:
        nib = np.empty((g, 128, n, 4), np.uint8)
        nib[..., 0::2] = words & 0xF
        nib[..., 1::2] = words >> 4
        vals = E2M1[nib]
    vals = vals * np.repeat(np.exp2(scales.astype(np.float64) - 127.0), 8, axis=1)[..., None]
    return vals.transpose(0, 1, 3, 2).reshape(g * 512, n)


def pack_table(v):
    words, scales = pack_weight(v, "e4m3")
    return np.concatenate([words.reshape(words.shape[0], -1), scales.reshape(scales.shape[0], -1)], axis=1)


def unpack_table(tab):
    g, t = tab.shape[0], tab.shape[1] // 528
    return unpack_weight(tab[:, :512 * t].reshape(g, 128, t, 4), tab[:, 512 * t:].reshape(g, 16, t), "e4m3")


K, L, M, T, S = 512, 1536, 256, 4096, 1024


def setup_inputs():
    n = np.random.standard_normal
    s1 = mx_kscale(K)[:, None]
    s2 = mx_kscale(L)[:, None]
    p_w4 = pack_weight(n((K, M)) / np.sqrt(K) / s1, "e2m1")
    return {
        "tab": pack_table(n((K, T)) * s1),
        "w4_words": p_w4[0],
        "w4_scales": p_w4[1],
        "x": (n((L, S)) * s2).astype(np.float32),
        "u": (n((L, M)) / np.sqrt(L) / s2).astype(np.float32),
        "b": (0.3 * n(256)).astype(np.float32),
        "offs": striped(np.random.permutation(T)[:S]),
    }


def reference(tab, w4_words, w4_scales, x, u, b, offs):
    tab_ = unpack_table(tab)[:, unstriped(offs)]
    w4_ = unpack_weight(w4_words, w4_scales, "e2m1")
    x_ = mxq(f64(x), 0, "e4m3")
    u_ = mxq(f64(u), 0, "e4m3")
    y = tab_.T @ w4_ + x_.T @ u_
    return y + f64(b)[None, :]

@@ -1,0 +1,194 @@
+from contextlib import ExitStack
+
+import concourse.mybir as mybir
+from concourse.masks import make_identity
+
+K, L, M, T, S = 512, 1536, 256, 4096, 1024
+FLOPS = 2 * S * M * (K + L)
+
+F32 = mybir.dt.float32
+BF16 = mybir.dt.bfloat16
+I32 = mybir.dt.int32
+U32 = mybir.dt.uint32
+U16 = mybir.dt.uint16
+U8 = mybir.dt.uint8
+E4M3 = mybir.dt.float8_e4m3fn_x4
+E2M1 = mybir.dt.float4_e2m1fn_x4
+ADD = mybir.AluOpType.add
+
+P = 128
+PACK = 4
+K_PASS = P * PACK
+PASSES = L // K_PASS
+CHUNK = 256
+CHUNKS = S // CHUNK
+N_TILE = 128
+
+
+def tile_list_tabx_tm_bias_kernel(tc, tab, w4_words, w4_scales, x, u, b, offs, out):
+    nc = tc.nc
+    with ExitStack() as ctx:
+        keep = ctx.enter_context(tc.tile_pool(name="keep", bufs=1))
+        psum = ctx.enter_context(tc.psum_pool(name="psum", bufs=8))
+
+        def held(shape, dtype, name):
+            return keep.tile(shape, dtype, name=name, align_bytes=64)
+
+        offsets = keep.tile([P, S // 16], U16, name="offsets")
+        tab_words = held([P, T], I32, "tab_words")
+        tab_scales = held([P, T // 4], I32, "tab_scales")
+        w4_codes = held([P, 2 * M], U8, "w4_codes")
+        w4_plane = held([P, M // 4], I32, "w4_plane")
+        b_col = held([P, 2], F32, "b_col")
+        u_raw = [held([P, PACK, M], F32, "u_raw%d" % g) for g in range(PASSES)]
+        x_raw = [held([P, PACK, S], F32, "x_raw%d" % g) for g in range(PASSES)]
+
+        for g in range(PASSES):
+            rows = u[g * K_PASS : (g + 1) * K_PASS, :]
+            nc.sync.dma_start(u_raw[g][:], rows.rearrange("(p i) n -> p i n", i=PACK))
+        nc.sync.dma_start(offsets[:], offs)
+        nc.sync.dma_start(tab_words[:], tab[0, 0 : 4 * P * T].rearrange("(p w) -> p w", p=P).bitcast(I32))
+        cuts = [[(0, S)], [(0, S)], [(0, 512), (512, 768), (768, 1024)]]
+        for g in range(PASSES):
+            rows = x[g * K_PASS : (g + 1) * K_PASS, :].rearrange("(p i) j -> p i j", i=PACK)
+            for lo, hi in cuts[g]:
+                nc.sync.dma_start(x_raw[g][:, :, lo:hi], rows[:, :, lo:hi])
+
+        nc.vector.memset(tab_scales[:], 0)
+        nc.vector.memset(w4_plane[:], 0)
+        nc.scalar.dma_start(b_col[:], b.rearrange("(p c) -> p c", c=2))
+        nc.scalar.dma_start(w4_codes[:].bitcast(I32), w4_words[0].bitcast(I32))
+        scale_rows = tab[0, 4 * P * T :].rearrange("(q t) -> q t", q=16)
+        for q in range(4):
+            nc.scalar.dma_start(tab_scales[32 * q : 32 * q + 4, :], scale_rows[4 * q : 4 * q + 4, :].bitcast(I32))
+        for q in range(4):
+            nc.scalar.dma_start(w4_plane[32 * q : 32 * q + 4, :], w4_scales[0][4 * q : 4 * q + 4, :].bitcast(I32))
+
+        ident = held([P, P], F32, "ident")
+        make_identity(nc, ident[:])
+        bias_bank = psum.tile([P, 2, P], F32, name="bank")
+        for c in range(2):
+            nc.tensor.transpose(bias_bank[:, c, :], b_col[:, c : c + 1].to_broadcast([P, P]), ident[:])
+        bias = held([P, M], F32, "bias")
+        nc.vector.tensor_copy(bias[:].rearrange("p (n c) -> p n c", c=2), bias_bank[:].rearrange("p c n -> p n c"))
+
+        def interleave(copy, grouped, raw):
+            copy(grouped.rearrange("p (c i) t -> p c t i", i=4), raw.rearrange("p t (c i) -> p c t i", i=4))
+
+        def quantize(codes, plane, grouped):
+            nc.vector.quantize_mx(out=codes.bitcast(E4M3), scales=plane, in_=grouped.rearrange("p w t -> p (w t)"))
+
+        u_codes, u_plane, u_grouped = [], [], []
+        for g in range(PASSES):
+            u_codes.append(held([P, M], U32, "u_codes%d" % g))
+            u_plane.append(held([P, M], U8, "u_plane%d" % g))
+            u_grouped.append(held([P, M, PACK], BF16, "u_grouped%d" % g))
+            interleave(nc.vector.tensor_copy if g == 1 else nc.scalar.copy, u_grouped[g][:], u_raw[g][:])
+        for g in range(PASSES):
+            quantize(u_codes[g][:], u_plane[g][:], u_grouped[g][:])
+
+        got_words = held([P, S], U32, "got_words")
+        got_scales = held([P, S], U8, "got_scales")
+        for lo in range(0, S, 512):
+            picks = offsets[:, lo // 16 : (lo + 512) // 16]
+            nc.vector.tensor_copy(got_words[:, lo : lo + 512], tab_words[:].bitcast(U32).indirect(picks))
+            nc.vector.tensor_copy(got_scales[:, lo : lo + 512], tab_scales[:].bitcast(U8).indirect(picks))
+
+        x_codes = [held([P, S], U32, "x_codes%d" % g) for g in range(PASSES)]
+        x_plane = [held([P, S], U8, "x_plane%d" % g) for g in range(PASSES)]
+        x_grouped = [[held([P, CHUNK, PACK], BF16, "x_grouped%d_%d" % (g, c)) for c in range(CHUNKS)] for g in range(PASSES)]
+
+        def interleave_chunk(g, c, vector_tokens):
+            base = c * CHUNK
+            if vector_tokens < CHUNK:
+                interleave(nc.scalar.copy, x_grouped[g][c][:, vector_tokens:, :], x_raw[g][:, :, base + vector_tokens : base + CHUNK])
+            if vector_tokens > 0:
+                interleave(nc.vector.tensor_copy, x_grouped[g][c][:, 0:vector_tokens, :], x_raw[g][:, :, base : base + vector_tokens])
+
+        def quantize_chunk(g, c):
+            cols = slice(c * CHUNK, (c + 1) * CHUNK)
+            quantize(x_codes[g][:, cols], x_plane[g][:, cols], x_grouped[g][c][:])
+
+        vector_share = [[0, 0, 0, 0], [0, 256, 0, 256], [0, 0, 128, 128]]
+        for g in range(2):
+            for c in range(CHUNKS):
+                interleave_chunk(g, c, vector_share[g][c])
+            for c in range(CHUNKS):
+                quantize_chunk(g, c)
+
+        acc = {}
+
+        def table_pass(t, h):
+            acc[t, h] = psum.tile([P, N_TILE], F32, name="bank")
+            tok = slice(t * P, (t + 1) * P)
+            nc.tensor.matmul_mx(
+                out=acc[t, h][:],
+                lhsT=got_words[:, tok].bitcast(E4M3),
+                lhsT_scale=got_scales[:, tok],
+                rhs=w4_codes[:, 2 * N_TILE * h : 2 * N_TILE * (h + 1)].bitcast(E2M1),
+                rhs_scale=w4_plane[:].bitcast(U8)[:, N_TILE * h : N_TILE * (h + 1)],
+                start=True,
+                stop=False,
+            )
+
+        def x_pass(g, t, h):
+            tok = slice(t * P, (t + 1) * P)
+            col = slice(h * N_TILE, (h + 1) * N_TILE)
+            nc.tensor.matmul_mx(
+                out=acc[t, h][:],
+                lhsT=x_codes[g][:, tok].bitcast(E4M3),
+                lhsT_scale=x_plane[g][:, tok],
+                rhs=u_codes[g][:, col].bitcast(E4M3),
+                rhs_scale=u_plane[g][:, col],
+                start=False,
+                stop=(g == PASSES - 1),
+            )
+
+        def open_groups(tiles):
+            groups = [(t, h) for t in tiles for h in range(2)]
+            for t, h in groups:
+                table_pass(t, h)
+            for g in range(PASSES - 1):
+                for t, h in groups:
+                    x_pass(g, t, h)
+
+        result = held([P, S // P, M], F32, "result")
+        out_tiles = out.rearrange("(t p) n -> p t n", p=P)
+
+        def close_groups(tiles):
+            for t in tiles:
+                for h in range(2):
+                    x_pass(PASSES - 1, t, h)
+
+        def add_bias(tiles):
+            for t in tiles:
+                for h in range(2):
+                    col = slice(h * N_TILE, (h + 1) * N_TILE)
+                    nc.vector.tensor_tensor(result[:, t, col], acc[t, h][:], bias[:, col], ADD)
+
+        def store(lo, hi):
+            nc.sync.dma_start(out_tiles[:, lo:hi, :], result[:, lo:hi, :])
+
+        open_groups(range(0, 4))
+        for c in range(2):
+            interleave_chunk(2, c, vector_share[2][c])
+        for c in range(2):
+            quantize_chunk(2, c)
+            close_groups((2 * c, 2 * c + 1))
+        interleave_chunk(2, 2, vector_share[2][2])
+        quantize_chunk(2, 2)
+        add_bias((0, 1))
+        store(0, 2)
+        add_bias((2, 3))
+        store(2, 4)
+        open_groups(range(4, 8))
+        close_groups((4, 5))
+        interleave_chunk(2, 3, vector_share[2][3])
+        quantize_chunk(2, 3)
+        close_groups((6, 7))
+        add_bias((4, 5))
+        store(4, 6)
+        add_bias((6,))
+        store(6, 7)
+        add_bias((7,))
+        store(7, 8)

@@ -20,9 +20,8 @@ P = 128
 PACK = 4
 K_PASS = P * PACK
 PASSES = L // K_PASS
-CHUNK = 256
-CHUNKS = S // CHUNK
 N_TILE = 128
+LAST = 768
 
 
 def tile_list_tabx_tm_bias_kernel(tc, tab, w4_words, w4_scales, x, u, b, offs, out):
@@ -40,29 +39,71 @@ def tile_list_tabx_tm_bias_kernel(tc, tab, w4_words, w4_scales, x, u, b, offs, o
         w4_codes = held([P, 2 * M], U8, "w4_codes")
         w4_plane = held([P, M // 4], I32, "w4_plane")
         b_col = held([P, 2], F32, "b_col")
-        u_raw = [held([P, PACK, M], F32, "u_raw%d" % g) for g in range(PASSES)]
-        x_raw = [held([P, PACK, S], F32, "x_raw%d" % g) for g in range(PASSES)]
+        u_raw = held([P, PASSES, PACK, M], F32, "u_raw")
+        x_raw = held([P, PASSES, PACK, S], F32, "x_raw")
 
-        for g in range(PASSES):
+        def load_u(g):
             rows = u[g * K_PASS : (g + 1) * K_PASS, :]
-            nc.sync.dma_start(u_raw[g][:], rows.rearrange("(p i) n -> p i n", i=PACK))
+            nc.sync.dma_start(u_raw[:, g], rows.rearrange("(p i) n -> p i n", i=PACK))
+
+        def load_x(g, lo, hi):
+            rows = x[g * K_PASS : (g + 1) * K_PASS, :].rearrange("(p i) j -> p i j", i=PACK)
+            nc.sync.dma_start(x_raw[:, g, :, lo:hi], rows[:, :, lo:hi])
+
+        load_u(0)
+        load_u(1)
         nc.sync.dma_start(offsets[:], offs)
         nc.sync.dma_start(tab_words[:], tab[0, 0 : 4 * P * T].rearrange("(p w) -> p w", p=P).bitcast(I32))
-        cuts = [[(0, S)], [(0, S)], [(0, 512), (512, 768), (768, 1024)]]
-        for g in range(PASSES):
-            rows = x[g * K_PASS : (g + 1) * K_PASS, :].rearrange("(p i) j -> p i j", i=PACK)
-            for lo, hi in cuts[g]:
-                nc.sync.dma_start(x_raw[g][:, :, lo:hi], rows[:, :, lo:hi])
-
+        nc.sync.dma_start(b_col[:], b.rearrange("(p c) -> p c", c=2))
+        nc.sync.dma_start(w4_codes[:].bitcast(I32), w4_words[0].bitcast(I32))
         nc.vector.memset(tab_scales[:], 0)
         nc.vector.memset(w4_plane[:], 0)
-        nc.scalar.dma_start(b_col[:], b.rearrange("(p c) -> p c", c=2))
-        nc.scalar.dma_start(w4_codes[:].bitcast(I32), w4_words[0].bitcast(I32))
+        nc.vector.memset(x_raw[:, :, 0, 0:S:P], 0.0)
+        nc.vector.memset(u_raw[:, 2, 0, 0:1], 0.0)
         scale_rows = tab[0, 4 * P * T :].rearrange("(q t) -> q t", q=16)
         for q in range(4):
-            nc.scalar.dma_start(tab_scales[32 * q : 32 * q + 4, :], scale_rows[4 * q : 4 * q + 4, :].bitcast(I32))
+            nc.sync.dma_start(tab_scales[32 * q : 32 * q + 4, :], scale_rows[4 * q : 4 * q + 4, :].bitcast(I32))
+        load_x(0, 0, S)
         for q in range(4):
-            nc.scalar.dma_start(w4_plane[32 * q : 32 * q + 4, :], w4_scales[0][4 * q : 4 * q + 4, :].bitcast(I32))
+            nc.sync.dma_start(w4_plane[32 * q : 32 * q + 4, :], w4_scales[0][4 * q : 4 * q + 4, :].bitcast(I32))
+        load_u(2)
+        load_x(1, 0, 512)
+        load_x(2, 0, 512)
+        load_x(1, 512, S)
+        load_x(2, 512, LAST)
+        load_x(2, LAST, S)
+
+        def interleave(copy, grouped, raw):
+            copy(grouped.rearrange("p (c i) t -> p c t i", i=4), raw.rearrange("p t (c i) -> p c t i", i=4))
+
+        def quantize(codes, plane, grouped):
+            nc.vector.quantize_mx(out=codes.bitcast(E4M3), scales=plane, in_=grouped.rearrange("p w t -> p (w t)"))
+
+        u_codes = [held([P, M], U32, "u_codes%d" % g) for g in range(PASSES)]
+        u_plane = [held([P, M], U8, "u_plane%d" % g) for g in range(PASSES)]
+        u_grouped = [held([P, M, PACK], BF16, "u_grouped%d" % g) for g in range(PASSES)]
+
+        def quantize_u(g):
+            quantize(u_codes[g][:], u_plane[g][:], u_grouped[g][:])
+
+        x_codes = [held([P, S], U32, "x_codes%d" % g) for g in range(PASSES)]
+        x_plane = [held([P, S], U8, "x_plane%d" % g) for g in range(PASSES)]
+        x_grouped = [held([P, S, PACK], BF16, "x_grouped%d" % g) for g in range(PASSES)]
+
+        def interleave_x(g, lo, hi, vector_tokens):
+            mid = hi - vector_tokens
+            if lo < mid:
+                interleave(nc.scalar.copy, x_grouped[g][:, lo:mid, :], x_raw[:, g, :, lo:mid])
+            if mid < hi:
+                interleave(nc.vector.tensor_copy, x_grouped[g][:, mid:hi, :], x_raw[:, g, :, mid:hi])
+
+        def quantize_x(g, lo, hi):
+            quantize(x_codes[g][:, lo:hi], x_plane[g][:, lo:hi], x_grouped[g][:, lo:hi, :])
+
+        interleave(nc.scalar.copy, u_grouped[0][:], u_raw[:, 0])
+        interleave(nc.scalar.copy, u_grouped[1][:], u_raw[:, 1])
+        quantize_u(0)
+        quantize_u(1)
 
         ident = held([P, P], F32, "ident")
         make_identity(nc, ident[:])
@@ -72,49 +113,12 @@ def tile_list_tabx_tm_bias_kernel(tc, tab, w4_words, w4_scales, x, u, b, offs, o
         bias = held([P, M], F32, "bias")
         nc.vector.tensor_copy(bias[:].rearrange("p (n c) -> p n c", c=2), bias_bank[:].rearrange("p c n -> p n c"))
 
-        def interleave(copy, grouped, raw):
-            copy(grouped.rearrange("p (c i) t -> p c t i", i=4), raw.rearrange("p t (c i) -> p c t i", i=4))
-
-        def quantize(codes, plane, grouped):
-            nc.vector.quantize_mx(out=codes.bitcast(E4M3), scales=plane, in_=grouped.rearrange("p w t -> p (w t)"))
-
-        u_codes, u_plane, u_grouped = [], [], []
-        for g in range(PASSES):
-            u_codes.append(held([P, M], U32, "u_codes%d" % g))
-            u_plane.append(held([P, M], U8, "u_plane%d" % g))
-            u_grouped.append(held([P, M, PACK], BF16, "u_grouped%d" % g))
-            interleave(nc.vector.tensor_copy if g == 1 else nc.scalar.copy, u_grouped[g][:], u_raw[g][:])
-        for g in range(PASSES):
-            quantize(u_codes[g][:], u_plane[g][:], u_grouped[g][:])
-
         got_words = held([P, S], U32, "got_words")
         got_scales = held([P, S], U8, "got_scales")
         for lo in range(0, S, 512):
             picks = offsets[:, lo // 16 : (lo + 512) // 16]
             nc.vector.tensor_copy(got_words[:, lo : lo + 512], tab_words[:].bitcast(U32).indirect(picks))
             nc.vector.tensor_copy(got_scales[:, lo : lo + 512], tab_scales[:].bitcast(U8).indirect(picks))
-
-        x_codes = [held([P, S], U32, "x_codes%d" % g) for g in range(PASSES)]
-        x_plane = [held([P, S], U8, "x_plane%d" % g) for g in range(PASSES)]
-        x_grouped = [[held([P, CHUNK, PACK], BF16, "x_grouped%d_%d" % (g, c)) for c in range(CHUNKS)] for g in range(PASSES)]
-
-        def interleave_chunk(g, c, vector_tokens):
-            base = c * CHUNK
-            if vector_tokens < CHUNK:
-                interleave(nc.scalar.copy, x_grouped[g][c][:, vector_tokens:, :], x_raw[g][:, :, base + vector_tokens : base + CHUNK])
-            if vector_tokens > 0:
-                interleave(nc.vector.tensor_copy, x_grouped[g][c][:, 0:vector_tokens, :], x_raw[g][:, :, base : base + vector_tokens])
-
-        def quantize_chunk(g, c):
-            cols = slice(c * CHUNK, (c + 1) * CHUNK)
-            quantize(x_codes[g][:, cols], x_plane[g][:, cols], x_grouped[g][c][:])
-
-        vector_share = [[0, 0, 0, 0], [0, 256, 0, 256], [0, 0, 128, 128]]
-        for g in range(2):
-            for c in range(CHUNKS):
-                interleave_chunk(g, c, vector_share[g][c])
-            for c in range(CHUNKS):
-                quantize_chunk(g, c)
 
         acc = {}
 
@@ -144,21 +148,18 @@ def tile_list_tabx_tm_bias_kernel(tc, tab, w4_words, w4_scales, x, u, b, offs, o
                 stop=(g == PASSES - 1),
             )
 
-        def open_groups(tiles):
-            groups = [(t, h) for t in tiles for h in range(2)]
-            for t, h in groups:
-                table_pass(t, h)
-            for g in range(PASSES - 1):
-                for t, h in groups:
+        def table_passes(tiles):
+            for t in tiles:
+                for h in range(2):
+                    table_pass(t, h)
+
+        def x_passes(g, tiles):
+            for t in tiles:
+                for h in range(2):
                     x_pass(g, t, h)
 
         result = held([P, S // P, M], F32, "result")
         out_tiles = out.rearrange("(t p) n -> p t n", p=P)
-
-        def close_groups(tiles):
-            for t in tiles:
-                for h in range(2):
-                    x_pass(PASSES - 1, t, h)
 
         def add_bias(tiles):
             for t in tiles:
@@ -169,23 +170,40 @@ def tile_list_tabx_tm_bias_kernel(tc, tab, w4_words, w4_scales, x, u, b, offs, o
         def store(lo, hi):
             nc.sync.dma_start(out_tiles[:, lo:hi, :], result[:, lo:hi, :])
 
-        open_groups(range(0, 4))
-        for c in range(2):
-            interleave_chunk(2, c, vector_share[2][c])
-        for c in range(2):
-            quantize_chunk(2, c)
-            close_groups((2 * c, 2 * c + 1))
-        interleave_chunk(2, 2, vector_share[2][2])
-        quantize_chunk(2, 2)
+        early, late = range(0, 4), range(4, 8)
+
+        table_passes(early)
+        for lo in range(0, S, 256):
+            interleave_x(0, lo, lo + 256, 64)
+            quantize_x(0, lo, lo + 256)
+        x_passes(0, early)
+        interleave(nc.scalar.copy, u_grouped[2][:], u_raw[:, 2])
+        quantize_u(2)
+        for lo in range(0, 512, 256):
+            interleave_x(1, lo, lo + 256, 64)
+            quantize_x(1, lo, lo + 256)
+        x_passes(1, early)
+        for lo in range(0, 512, 256):
+            interleave_x(2, lo, lo + 256, 96)
+            quantize_x(2, lo, lo + 256)
+            x_passes(2, range(lo // P, lo // P + 2))
+        for lo in range(512, S, 256):
+            interleave_x(1, lo, lo + 256, 64)
         add_bias((0, 1))
         store(0, 2)
         add_bias((2, 3))
         store(2, 4)
-        open_groups(range(4, 8))
-        close_groups((4, 5))
-        interleave_chunk(2, 3, vector_share[2][3])
-        quantize_chunk(2, 3)
-        close_groups((6, 7))
+        for lo in range(512, S, 256):
+            quantize_x(1, lo, lo + 256)
+        table_passes(late)
+        x_passes(0, late)
+        x_passes(1, late)
+        interleave_x(2, 512, LAST, 96)
+        quantize_x(2, 512, LAST)
+        x_passes(2, (4, 5))
+        interleave_x(2, LAST, S, 96)
+        quantize_x(2, LAST, S)
+        x_passes(2, (6, 7))
         add_bias((4, 5))
         store(4, 6)
         add_bias((6,))

@@ -60,12 +60,13 @@ def tile_list_tabx_tm_bias_kernel(tc, tab, w4_words, w4_scales, x, u, b, offs, o
         nc.vector.memset(w4_plane[:], 0)
         nc.vector.memset(x_raw[:, :, 0, 0:S:P], 0.0)
         nc.vector.memset(u_raw[:, 2, 0, 0:1], 0.0)
-        scale_rows = tab[0, 4 * P * T :].rearrange("(q t) -> q t", q=16)
-        for q in range(4):
-            nc.sync.dma_start(tab_scales[32 * q : 32 * q + 4, :], scale_rows[4 * q : 4 * q + 4, :].bitcast(I32))
+        scale_rows = tab[0, 4 * P * T :].rearrange("(q r t) -> r q t", q=4, r=4)
+        for r in range(4):
+            nc.sync.dma_start(tab_scales[r:P:32, :], scale_rows[r].bitcast(I32))
         load_x(0, 0, S)
-        for q in range(4):
-            nc.sync.dma_start(w4_plane[32 * q : 32 * q + 4, :], w4_scales[0][4 * q : 4 * q + 4, :].bitcast(I32))
+        w4_scale_rows = w4_scales[0].rearrange("(q r) n -> r q n", r=4)
+        for r in range(4):
+            nc.sync.dma_start(w4_plane[r:P:32, :], w4_scale_rows[r].bitcast(I32))
         load_u(2)
         load_x(1, 0, 512)
         load_x(2, 0, 512)
@@ -180,7 +181,7 @@ def tile_list_tabx_tm_bias_kernel(tc, tab, w4_words, w4_scales, x, u, b, offs, o
         interleave(nc.scalar.copy, u_grouped[2][:], u_raw[:, 2])
         quantize_u(2)
         for lo in range(0, 512, 256):
-            interleave_x(1, lo, lo + 256, 64)
+            interleave_x(1, lo, lo + 256, 80)
             quantize_x(1, lo, lo + 256)
         x_passes(1, early)
         for lo in range(0, 512, 256):

from contextlib import ExitStack

import concourse.mybir as mybir
from concourse.masks import make_identity

K, L, M, T, S = 512, 1536, 256, 4096, 1024
FLOPS = 2 * S * M * (K + L)

F32 = mybir.dt.float32
BF16 = mybir.dt.bfloat16
I32 = mybir.dt.int32
U32 = mybir.dt.uint32
U16 = mybir.dt.uint16
U8 = mybir.dt.uint8
E4M3 = mybir.dt.float8_e4m3fn_x4
E2M1 = mybir.dt.float4_e2m1fn_x4
ADD = mybir.AluOpType.add

P = 128
PACK = 4
K_PASS = P * PACK
PASSES = L // K_PASS
N_TILE = 128
LAST = 768


def tile_list_tabx_tm_bias_kernel(tc, tab, w4_words, w4_scales, x, u, b, offs, out):
    nc = tc.nc
    with ExitStack() as ctx:
        keep = ctx.enter_context(tc.tile_pool(name="keep", bufs=1))
        psum = ctx.enter_context(tc.psum_pool(name="psum", bufs=8))

        def held(shape, dtype, name):
            return keep.tile(shape, dtype, name=name, align_bytes=64)

        offsets = keep.tile([P, S // 16], U16, name="offsets")
        tab_words = held([P, T], I32, "tab_words")
        tab_scales = held([P, T // 4], I32, "tab_scales")
        w4_codes = held([P, 2 * M], U8, "w4_codes")
        w4_plane = held([P, M // 4], I32, "w4_plane")
        b_col = held([P, 2], F32, "b_col")
        u_raw = held([P, PASSES, PACK, M], F32, "u_raw")
        x_raw = held([P, PASSES, PACK, S], F32, "x_raw")

        def load_u(g):
            rows = u[g * K_PASS : (g + 1) * K_PASS, :]
            nc.sync.dma_start(u_raw[:, g], rows.rearrange("(p i) n -> p i n", i=PACK))

        def load_x(g, lo, hi):
            rows = x[g * K_PASS : (g + 1) * K_PASS, :].rearrange("(p i) j -> p i j", i=PACK)
            nc.sync.dma_start(x_raw[:, g, :, lo:hi], rows[:, :, lo:hi])

        load_u(0)
        load_u(1)
        nc.sync.dma_start(offsets[:], offs)
        nc.sync.dma_start(tab_words[:], tab[0, 0 : 4 * P * T].rearrange("(p w) -> p w", p=P).bitcast(I32))
        nc.sync.dma_start(b_col[:], b.rearrange("(p c) -> p c", c=2))
        nc.sync.dma_start(w4_codes[:].bitcast(I32), w4_words[0].bitcast(I32))
        nc.vector.memset(tab_scales[:], 0)
        nc.vector.memset(w4_plane[:], 0)
        nc.vector.memset(x_raw[:, :, 0, 0:S:P], 0.0)
        nc.vector.memset(u_raw[:, 2, 0, 0:1], 0.0)
        scale_rows = tab[0, 4 * P * T :].rearrange("(q r t) -> r q t", q=4, r=4)
        for r in range(4):
            nc.sync.dma_start(tab_scales[r:P:32, :], scale_rows[r].bitcast(I32))
        load_x(0, 0, S)
        w4_scale_rows = w4_scales[0].rearrange("(q r) n -> r q n", r=4)
        for r in range(4):
            nc.sync.dma_start(w4_plane[r:P:32, :], w4_scale_rows[r].bitcast(I32))
        load_u(2)
        load_x(1, 0, 512)
        load_x(2, 0, 512)
        load_x(1, 512, S)
        load_x(2, 512, LAST)
        load_x(2, LAST, S)

        def interleave(copy, grouped, raw):
            copy(grouped.rearrange("p (c i) t -> p c t i", i=4), raw.rearrange("p t (c i) -> p c t i", i=4))

        def quantize(codes, plane, grouped):
            nc.vector.quantize_mx(out=codes.bitcast(E4M3), scales=plane, in_=grouped.rearrange("p w t -> p (w t)"))

        u_codes = [held([P, M], U32, "u_codes%d" % g) for g in range(PASSES)]
        u_plane = [held([P, M], U8, "u_plane%d" % g) for g in range(PASSES)]
        u_grouped = [held([P, M, PACK], BF16, "u_grouped%d" % g) for g in range(PASSES)]

        def quantize_u(g):
            quantize(u_codes[g][:], u_plane[g][:], u_grouped[g][:])

        x_codes = [held([P, S], U32, "x_codes%d" % g) for g in range(PASSES)]
        x_plane = [held([P, S], U8, "x_plane%d" % g) for g in range(PASSES)]
        x_grouped = [held([P, S, PACK], BF16, "x_grouped%d" % g) for g in range(PASSES)]

        def interleave_x(g, lo, hi, vector_tokens):
            mid = hi - vector_tokens
            if lo < mid:
                interleave(nc.scalar.copy, x_grouped[g][:, lo:mid, :], x_raw[:, g, :, lo:mid])
            if mid < hi:
                interleave(nc.vector.tensor_copy, x_grouped[g][:, mid:hi, :], x_raw[:, g, :, mid:hi])

        def quantize_x(g, lo, hi):
            quantize(x_codes[g][:, lo:hi], x_plane[g][:, lo:hi], x_grouped[g][:, lo:hi, :])

        interleave(nc.scalar.copy, u_grouped[0][:], u_raw[:, 0])
        interleave(nc.scalar.copy, u_grouped[1][:], u_raw[:, 1])
        quantize_u(0)
        quantize_u(1)

        ident = held([P, P], F32, "ident")
        make_identity(nc, ident[:])
        bias_bank = psum.tile([P, 2, P], F32, name="bank")
        for c in range(2):
            nc.tensor.transpose(bias_bank[:, c, :], b_col[:, c : c + 1].to_broadcast([P, P]), ident[:])
        bias = held([P, M], F32, "bias")
        nc.vector.tensor_copy(bias[:].rearrange("p (n c) -> p n c", c=2), bias_bank[:].rearrange("p c n -> p n c"))

        got_words = held([P, S], U32, "got_words")
        got_scales = held([P, S], U8, "got_scales")
        for lo in range(0, S, 512):
            picks = offsets[:, lo // 16 : (lo + 512) // 16]
            nc.vector.tensor_copy(got_words[:, lo : lo + 512], tab_words[:].bitcast(U32).indirect(picks))
            nc.vector.tensor_copy(got_scales[:, lo : lo + 512], tab_scales[:].bitcast(U8).indirect(picks))

        acc = {}

        def table_pass(t, h):
            acc[t, h] = psum.tile([P, N_TILE], F32, name="bank")
            tok = slice(t * P, (t + 1) * P)
            nc.tensor.matmul_mx(
                out=acc[t, h][:],
                lhsT=got_words[:, tok].bitcast(E4M3),
                lhsT_scale=got_scales[:, tok],
                rhs=w4_codes[:, 2 * N_TILE * h : 2 * N_TILE * (h + 1)].bitcast(E2M1),
                rhs_scale=w4_plane[:].bitcast(U8)[:, N_TILE * h : N_TILE * (h + 1)],
                start=True,
                stop=False,
            )

        def x_pass(g, t, h):
            tok = slice(t * P, (t + 1) * P)
            col = slice(h * N_TILE, (h + 1) * N_TILE)
            nc.tensor.matmul_mx(
                out=acc[t, h][:],
                lhsT=x_codes[g][:, tok].bitcast(E4M3),
                lhsT_scale=x_plane[g][:, tok],
                rhs=u_codes[g][:, col].bitcast(E4M3),
                rhs_scale=u_plane[g][:, col],
                start=False,
                stop=(g == PASSES - 1),
            )

        def table_passes(tiles):
            for t in tiles:
                for h in range(2):
                    table_pass(t, h)

        def x_passes(g, tiles):
            for t in tiles:
                for h in range(2):
                    x_pass(g, t, h)

        result = held([P, S // P, M], F32, "result")
        out_tiles = out.rearrange("(t p) n -> p t n", p=P)

        def add_bias(tiles):
            for t in tiles:
                for h in range(2):
                    col = slice(h * N_TILE, (h + 1) * N_TILE)
                    nc.vector.tensor_tensor(result[:, t, col], acc[t, h][:], bias[:, col], ADD)

        def store(lo, hi):
            nc.sync.dma_start(out_tiles[:, lo:hi, :], result[:, lo:hi, :])

        early, late = range(0, 4), range(4, 8)

        table_passes(early)
        for lo in range(0, S, 256):
            interleave_x(0, lo, lo + 256, 64)
            quantize_x(0, lo, lo + 256)
        x_passes(0, early)
        interleave(nc.scalar.copy, u_grouped[2][:], u_raw[:, 2])
        quantize_u(2)
        for lo in range(0, 512, 256):
            interleave_x(1, lo, lo + 256, 80)
            quantize_x(1, lo, lo + 256)
        x_passes(1, early)
        for lo in range(0, 512, 256):
            interleave_x(2, lo, lo + 256, 96)
            quantize_x(2, lo, lo + 256)
            x_passes(2, range(lo // P, lo // P + 2))
        for lo in range(512, S, 256):
            interleave_x(1, lo, lo + 256, 64)
        add_bias((0, 1))
        store(0, 2)
        add_bias((2, 3))
        store(2, 4)
        for lo in range(512, S, 256):
            quantize_x(1, lo, lo + 256)
        table_passes(late)
        x_passes(0, late)
        x_passes(1, late)
        interleave_x(2, 512, LAST, 96)
        quantize_x(2, 512, LAST)
        x_passes(2, (4, 5))
        interleave_x(2, LAST, S, 96)
        quantize_x(2, LAST, S)
        x_passes(2, (6, 7))
        add_bias((4, 5))
        store(4, 6)
        add_bias((6,))
        store(6, 7)
        add_bias((7,))
        store(7, 8)
